import numpy as np
import ml_dtypes


def mxq(x, axis, fmt="e4m3"):
    dtype, down = {"e4m3": (ml_dtypes.float8_e4m3fn, 7), "e5m2": (ml_dtypes.float8_e5m2, 14)}[fmt]
    v = np.moveaxis(np.asarray(x, np.float32).astype(ml_dtypes.bfloat16).astype(np.float64), axis, -1)
    blocks = v.reshape(v.shape[:-1] + (-1, 32))
    amax = np.abs(blocks).max(-1, keepdims=True)
    byte = np.maximum(np.where(amax > 0, np.frexp(amax)[1] - 1 + 127, 0) - down, 1)
    scale = np.exp2(byte - 127.0)
    codes = (blocks / scale).astype(np.float32).astype(dtype).astype(np.float64)
    return np.moveaxis((codes * scale).reshape(v.shape), -1, axis)


WIDE = False


def mx_kscale(k):
    if not WIDE:
        return np.ones(k)
    levels = np.array([10, -10, 5, -5, 0])
    if k % 512:
        return np.exp2(np.random.permutation(np.resize(levels, k // 32))).repeat(32)
    a = np.empty((k // 512, 16))
    for p in range(k // 512):
        a[p, :8] = np.random.permutation(np.resize(levels, 8))
        for g in range(8):
            far = levels[np.abs(levels - a[p, g]) >= 10]
            a[p, g + 8] = far[np.random.randint(len(far))]
    return np.exp2(a.ravel()).repeat(32)


def f64(x):
    return np.asarray(x).astype(np.float64)


def striped(idx):
    return np.tile(idx.reshape(-1, 16).T, (8, 1)).astype(np.uint16)


def unstriped(offs):
    return offs[:16].T.reshape(-1).astype(np.int64)


def striped8(idx):
    return np.concatenate([x.reshape(-1, 16).T for x in idx]).astype(np.uint16)


def runs(offs, k):
    lists = np.stack([offs[16 * r : 16 * r + 16].T.reshape(-1) for r in range(8)]).astype(np.int64)
    return lists[np.arange(k) % 512 // 64]


def pack_weight(w):
    k, n = w.shape
    w = f64(np.asarray(w, np.float32).astype(ml_dtypes.bfloat16)).reshape(k // 32, 32, n)
    amax = np.abs(w).max(1)
    byte = np.clip(np.where(amax > 0, np.frexp(amax)[1] - 1 + 127 - 7, 1), 1, 254)
    scaled = (w * np.exp2(127.0 - byte)[:, None, :]).reshape(k, n).astype(np.float32)
    words = np.ascontiguousarray(scaled.reshape(k // 512, 128, 4, n).transpose(0, 1, 3, 2)).astype(ml_dtypes.float8_e4m3fn).view(np.uint8)
    return words, np.ascontiguousarray(byte.astype(np.uint8).reshape(k // 512, 16, n))


def unpack_weight(words, scales):
    g, p, n, _ = words.shape
    vals = np.ascontiguousarray(words).view(ml_dtypes.float8_e4m3fn).astype(np.float64) * np.repeat(np.exp2(scales.astype(np.float64) - 127.0), 8, axis=1)[..., None]
    return vals.transpose(0, 1, 3, 2).reshape(g * 512, n)


K, T, S, N, H, W, U = 512, 2048, 512, 512, 512, 256, 1024


def setup_inputs():
    n = np.random.standard_normal
    s = mx_kscale(K)[:, None]
    u = mx_kscale(H)
    packed_xT = pack_weight(n((K, T)) * s)
    return {
        "x_words": packed_xT[0],
        "x_scales": packed_xT[1],
        "w1": (n((K, H)) / np.sqrt(K) / s).astype(np.float32),
        "w2": (n((K, H)) / np.sqrt(K) / s).astype(np.float32),
        "gn": (np.random.uniform(0.5, 1.5, (H, 1)) * u[:, None]).astype(np.float32),
        "w3": (n((H, N)) / np.sqrt(H) / u[:, None]).astype(np.float32),
        "mem": n((N, U)).astype(np.float32),
        "offs": striped(np.random.permutation(T)[:S]),
        "two": striped(np.random.permutation(T)[:S]),
        "n1": striped8(np.stack([np.random.permutation(S)[:W] for _ in range(8)])),
        "n2": striped8(np.stack([np.random.permutation(S)[:W] for _ in range(8)])),
        "n3": striped8(np.stack([np.random.permutation(U)[:S] for _ in range(8)])),
        "n4": striped8(np.stack([np.random.permutation(U) for _ in range(8)])),
    }


def reference(x_words, x_scales, w1, w2, gn, w3, mem, offs, two, n1, n2, n3, n4):
    x_two = unpack_weight(x_words, x_scales)[:, unstriped(two)]
    d = mxq(f64(w2), 0, "e4m3").T @ x_two
    xq = unpack_weight(x_words, x_scales)[:, unstriped(offs)]
    y = mxq(f64(w1), 0, "e4m3").T @ xq
    ra = d[np.arange(H)[:, None], runs(n2, H)] - (0.5 * (y[np.arange(H)[:, None], runs(n1, H)]))
    ds = y.copy()
    ds[np.arange(H)[:, None], runs(n1, H)] = ra
    z = f64(gn) * ds
    h = mxq(f64(w3), 0, "e4m3").T @ mxq(z, 0, "e4m3")
    pg = f64(mem).copy()
    pg[np.arange(N)[:, None], runs(n3, N)] = h
    return pg - (0.5 * (pg[np.arange(N)[:, None], runs(n4, N)]))

@@ -1,0 +1,198 @@
+from contextlib import ExitStack
+
+import concourse.mybir as mybir
+
+K, T, S, N, H, W, U = 512, 2048, 512, 512, 512, 256, 1024
+FLOPS = 2 * K * H * S * 2 + 2 * H * N * S
+
+F32 = mybir.dt.float32
+BF16 = mybir.dt.bfloat16
+I32 = mybir.dt.int32
+U32 = mybir.dt.uint32
+U16 = mybir.dt.uint16
+U8 = mybir.dt.uint8
+FP8X4 = mybir.dt.float8_e4m3fn_x4
+MULT = mybir.AluOpType.mult
+ADD = mybir.AluOpType.add
+COPY = mybir.ActivationFunctionType.Copy
+
+P = 128
+PACK = 4
+HALF = 256
+FIRST = 128
+
+
+def tile_picked_twlputbpagem_none_p_kernel(tc, x_words, x_scales, w1, w2, gn, w3, mem, offs, two, n1, n2, n3, n4, out):
+    nc = tc.nc
+    with ExitStack() as ctx:
+        lists = ctx.enter_context(tc.tile_pool(name="lists", bufs=1))
+        sb = ctx.enter_context(tc.tile_pool(name="sb", bufs=1))
+        psum = ctx.enter_context(tc.psum_pool(name="psum", bufs=1))
+
+        def load_list(src, name):
+            tile = lists.tile(list(src.shape), U16, name=name)
+            nc.sync.dma_start(tile[:], src)
+            return tile
+
+        def load_weight(w, name):
+            halves = []
+            for h in range(2):
+                raw = sb.tile([P, PACK, HALF], F32, name="%s_raw%d" % (name, h))
+                nc.sync.dma_start(raw[:], w[:, h * HALF : (h + 1) * HALF].rearrange("(p j) c -> p j c", j=PACK))
+                halves.append(raw)
+            return halves
+
+        def round_part(copy, grouped, raw, m0, c0, count):
+            dealt = grouped[:].rearrange("p (t m j) -> p m j t", t=PACK, j=PACK)
+            copy(dealt[:, m0 : m0 + count], raw[:].rearrange("p j (m t) -> p m j t", t=PACK)[:, c0 : c0 + count])
+
+        def quantize(grouped, name):
+            codes = sb.tile([P, 512], U32, name=name + "_codes", align_bytes=64)
+            scales = sb.tile([P, 512], U8, name=name + "_scales", align_bytes=64)
+            nc.vector.quantize_mx(out=codes[:].bitcast(FP8X4), scales=scales[:], in_=grouped[:])
+            return codes, scales
+
+        def product(acc, weight, t, codes, scales):
+            cols = slice(t * P, (t + 1) * P)
+            nc.tensor.matmul_mx(out=acc, lhsT=weight[0][:, cols].bitcast(FP8X4), lhsT_scale=weight[1][:, cols],
+                                rhs=codes.bitcast(FP8X4), rhs_scale=scales, start=True, stop=True)
+
+        two_t = load_list(two, "two_t")
+        offs_t = load_list(offs, "offs_t")
+        xs = sb.tile([P, T], U8, name="xs", align_bytes=64)
+        nc.vector.memset(xs[:].bitcast(I32), 0)
+        for q in range(4):
+            nc.sync.dma_start(xs[32 * q : 32 * q + 4, :].bitcast(I32), x_scales[0, 4 * q : 4 * q + 4, :].bitcast(I32))
+        xw = sb.tile([P, T], I32, name="xw", align_bytes=64)
+        nc.sync.dma_start(xw[:], x_words[0].rearrange("p c r -> p (c r)").bitcast(I32))
+        w2_raw = load_weight(w2, "w2")
+        w1_raw = load_weight(w1, "w1")
+        n2_t = load_list(n2, "n2_t")
+        n1_t = load_list(n1, "n1_t")
+        gain = sb.tile([P, PACK], F32, name="gain")
+        nc.sync.dma_start(gain[:], gn.rearrange("(p t) o -> p (t o)", t=PACK))
+        w3_raw = sb.tile([P, PACK, N], F32, name="w3_raw")
+        nc.sync.dma_start(w3_raw[:], w3.rearrange("(p j) c -> p j c", j=PACK))
+        n3_t = load_list(n3, "n3_t")
+        pg = []
+        for t in range(PACK):
+            page = sb.tile([P, U], F32, name="pg%d" % t)
+            nc.sync.dma_start(page[:], mem.rearrange("(p t) w -> p t w", t=PACK)[:, t, :])
+            pg.append(page)
+        n4_t = load_list(n4, "n4_t")
+
+        picked = {}
+        for name, lst in (("two", two_t), ("offs", offs_t)):
+            scales = sb.tile([P, S], U8, name=name + "_s", align_bytes=64)
+            nc.vector.tensor_copy(scales[:], xs[:].indirect(lst[:]))
+            picked[name + "_s"] = scales
+        for name, lst in (("two", two_t), ("offs", offs_t)):
+            words = sb.tile([P, S], U32, name=name + "_w", align_bytes=64)
+            nc.vector.tensor_copy(words[:], xw[:].bitcast(U32).indirect(lst[:]))
+            picked[name + "_w"] = words
+
+        w2_bf16 = sb.tile([P, PACK * H], BF16, name="w2_bf16", align_bytes=64)
+        w1_bf16 = sb.tile([P, PACK * H], BF16, name="w1_bf16", align_bytes=64)
+        w3_bf16 = sb.tile([P, PACK * N], BF16, name="w3_bf16", align_bytes=64)
+        round_part(nc.scalar.copy, w2_bf16, w2_raw[0], 0, 0, 64)
+        round_part(nc.scalar.copy, w2_bf16, w2_raw[1], 64, 0, 64)
+        round_part(nc.scalar.copy, w1_bf16, w1_raw[0], 0, 0, 64)
+        w2_q = quantize(w2_bf16, "w2")
+        round_part(nc.vector.tensor_copy, w1_bf16, w1_raw[1], 64, 0, 64)
+        d = []
+        for t in range(PACK):
+            acc = psum.tile([P, S], F32, name="bank%d" % t)
+            product(acc[:], w2_q, t, picked["two_w"][:], picked["two_s"][:])
+            row = sb.tile([P, S], F32, name="d%d" % t)
+            nc.scalar.copy(row[:], acc[:])
+            d.append(row)
+        w1_q = quantize(w1_bf16, "w1")
+        ds = []
+        for t in range(PACK):
+            acc = psum.tile([P, S], F32, name="bank%d" % (PACK + t))
+            product(acc[:], w1_q, t, picked["offs_w"][:], picked["offs_s"][:])
+            row = sb.tile([P, S], F32, name="ds%d" % t)
+            nc.scalar.copy(row[:], acc[:])
+            ds.append(row)
+
+        for m0 in range(0, P, 32):
+            round_part(nc.scalar.copy, w3_bf16, w3_raw, m0, m0, 32)
+
+        from_d = []
+        for t in range(PACK):
+            got = sb.tile([P, W], F32, name="from_d%d" % t)
+            nc.vector.tensor_copy(got[:], d[t][:].indirect(n2_t[:]))
+            from_d.append(got)
+
+        z = sb.tile([P, S, PACK], BF16, name="z", align_bytes=64)
+        from_y = []
+
+        def fetch_y(t):
+            got = sb.tile([P, W], F32, name="from_y%d" % t)
+            nc.vector.tensor_scalar(got[:], ds[t][:].indirect(n1_t[:]), -0.5, 0.0, MULT, ADD)
+            from_y.append(got)
+
+        def put_ra(t):
+            nc.vector.tensor_tensor(ds[t][:].indirect(n1_t[:]), from_d[t][:], from_y[t][:], ADD)
+            for a, b in ((0, S),) if t + 1 < PACK else ((0, FIRST), (FIRST, S)):
+                nc.scalar.activation(z[:, a:b, t], ds[t][:, a:b], COPY, scale=gain[:, t : t + 1])
+
+        fetch_y(0)
+        for t in range(PACK):
+            if t + 1 < PACK:
+                fetch_y(t + 1)
+            put_ra(t)
+        w3_q = quantize(w3_bf16, "w3")
+
+        z_flat = z[:].rearrange("p s t -> p (s t)")
+        def quantize_z(a, b):
+            codes = sb.tile([P, b - a], U32, name="z_codes%d" % a, align_bytes=64)
+            scales = sb.tile([P, b - a], U8, name="z_scales%d" % a, align_bytes=64)
+            nc.vector.quantize_mx(out=codes[:].bitcast(FP8X4), scales=scales[:], in_=z_flat[:, PACK * a : PACK * b])
+            return a, b, codes, scales
+
+        z_first = quantize_z(0, FIRST)
+        h_first = []
+        for t in range(PACK):
+            acc = psum.tile([P, FIRST], F32, name="bank%d" % t)
+            product(acc[:], w3_q, t, z_first[2][:], z_first[3][:])
+            row = sb.tile([P, FIRST], F32, name="h_first%d" % t)
+            if t == 0:
+                nc.vector.tensor_copy(row[:], acc[:])
+            else:
+                nc.scalar.copy(row[:], acc[:])
+            h_first.append(row)
+        nc.vector.tensor_copy(pg[0][:].indirect(n3_t[:, : FIRST // 16]), h_first[0][:])
+        z_rest = [quantize_z(128, 256), quantize_z(256, 512)]
+        h_rest = []
+        for t in range(PACK):
+            acc = psum.tile([P, S], F32, name="bank%d" % (PACK + t))
+            for a, b, codes, scales in z_rest:
+                product(acc[:, a:b], w3_q, t, codes[:], scales[:])
+            row = sb.tile([P, S - FIRST], F32, name="h_rest%d" % t)
+            nc.scalar.copy(row[:], acc[:, FIRST:])
+            h_rest.append(row)
+        for t in range(1, PACK):
+            nc.vector.tensor_copy(pg[t][:].indirect(n3_t[:, : FIRST // 16]), h_first[t][:])
+
+        half = []
+        out_rows = out.rearrange("(p t) w -> p t w", t=PACK)
+
+        def put_h(t):
+            nc.vector.tensor_copy(pg[t][:].indirect(n3_t[:, FIRST // 16 :]), h_rest[t][:])
+            scaled = sb.tile([P, U], F32, name="half%d" % t)
+            nc.scalar.mul(scaled[:], pg[t][:], -0.5)
+            half.append(scaled)
+
+        def finish(t):
+            cuts = (0, 512, 1024) if t + 1 < PACK else (0, 512, 768, 1024)
+            for a, b in zip(cuts[:-1], cuts[1:]):
+                res = sb.tile([P, b - a], F32, name="res%d_%d" % (t, a))
+                nc.vector.tensor_tensor(res[:], half[t][:].indirect(n4_t[:, a // 16 : b // 16]), pg[t][:, a:b], ADD)
+                nc.sync.dma_start(out_rows[:, t, a:b], res[:])
+
+        put_h(0)
+        for t in range(PACK):
+            if t + 1 < PACK:
+                put_h(t + 1)
+            finish(t)

@@ -38,7 +38,8 @@ def tile_picked_twlputbpagem_none_p_kernel(tc, x_words, x_scales, w1, w2, gn, w3
             halves = []
             for h in range(2):
                 raw = sb.tile([P, PACK, HALF], F32, name="%s_raw%d" % (name, h))
-                nc.sync.dma_start(raw[:], w[:, h * HALF : (h + 1) * HALF].rearrange("(p j) c -> p j c", j=PACK))
+                queue = nc.scalar if (name, h) == ("w2", 0) else nc.sync
+                queue.dma_start(raw[:], w[:, h * HALF : (h + 1) * HALF].rearrange("(p j) c -> p j c", j=PACK))
                 halves.append(raw)
             return halves
 
@@ -46,10 +47,11 @@ def tile_picked_twlputbpagem_none_p_kernel(tc, x_words, x_scales, w1, w2, gn, w3
             dealt = grouped[:].rearrange("p (t m j) -> p m j t", t=PACK, j=PACK)
             copy(dealt[:, m0 : m0 + count], raw[:].rearrange("p j (m t) -> p m j t", t=PACK)[:, c0 : c0 + count])
 
-        def quantize(grouped, name):
+        def quantize(grouped, name, step=512):
             codes = sb.tile([P, 512], U32, name=name + "_codes", align_bytes=64)
             scales = sb.tile([P, 512], U8, name=name + "_scales", align_bytes=64)
-            nc.vector.quantize_mx(out=codes[:].bitcast(FP8X4), scales=scales[:], in_=grouped[:])
+            for c in range(0, 512, step):
+                nc.vector.quantize_mx(out=codes[:, c : c + step].bitcast(FP8X4), scales=scales[:, c : c + step], in_=grouped[:, PACK * c : PACK * (c + step)])
             return codes, scales
 
         def product(acc, weight, t, codes, scales):
@@ -92,37 +94,45 @@ def tile_picked_twlputbpagem_none_p_kernel(tc, x_words, x_scales, w1, w2, gn, w3
             picked[name + "_w"] = words
 
         w2_bf16 = sb.tile([P, PACK * H], BF16, name="w2_bf16", align_bytes=64)
-        w1_bf16 = sb.tile([P, PACK * H], BF16, name="w1_bf16", align_bytes=64)
+        w1_bf16 = sb.tile([P, PACK * H], BF16, name="w1_bf16", tag="w1_bf16", align_bytes=64)
         w3_bf16 = sb.tile([P, PACK * N], BF16, name="w3_bf16", align_bytes=64)
         round_part(nc.scalar.copy, w2_bf16, w2_raw[0], 0, 0, 64)
         round_part(nc.scalar.copy, w2_bf16, w2_raw[1], 64, 0, 64)
         round_part(nc.scalar.copy, w1_bf16, w1_raw[0], 0, 0, 64)
-        w2_q = quantize(w2_bf16, "w2")
+        w2_q = quantize(w2_bf16, "w2", 256)
         round_part(nc.vector.tensor_copy, w1_bf16, w1_raw[1], 64, 0, 64)
-        d = []
-        for t in range(PACK):
-            acc = psum.tile([P, S], F32, name="bank%d" % t)
+        d = [sb.tile([P, S], F32, name="d%d" % t) for t in range(PACK)]
+
+        def make_d(t, bank):
+            acc = psum.tile([P, S], F32, name="bank%d" % bank)
             product(acc[:], w2_q, t, picked["two_w"][:], picked["two_s"][:])
-            row = sb.tile([P, S], F32, name="d%d" % t)
-            nc.scalar.copy(row[:], acc[:])
-            d.append(row)
-        w1_q = quantize(w1_bf16, "w1")
-        ds = []
-        for t in range(PACK):
-            acc = psum.tile([P, S], F32, name="bank%d" % (PACK + t))
-            product(acc[:], w1_q, t, picked["offs_w"][:], picked["offs_s"][:])
-            row = sb.tile([P, S], F32, name="ds%d" % t)
-            nc.scalar.copy(row[:], acc[:])
-            ds.append(row)
+            nc.scalar.copy(d[t][:], acc[:])
+
+        for t in range(PACK - 1):
+            make_d(t, t)
+        w1_q = quantize(w1_bf16, "w1", 256)
+        ds = [sb.tile([P, S], F32, name="ds%d" % t) for t in range(PACK)]
+        for t in range(0, PACK, 2):
+            later = psum.tile([P, S], F32, name="bank%d" % (PACK + t + 1))
+            product(later[:], w1_q, t + 1, picked["offs_w"][:], picked["offs_s"][:])
+            first = psum.tile([P, S], F32, name="bank%d" % (PACK + t))
+            product(first[:], w1_q, t, picked["offs_w"][:], picked["offs_s"][:])
+            nc.scalar.copy(ds[t + 1][:, :448], later[:, :448])
+            nc.scalar.copy(ds[t][:], first[:])
+            nc.scalar.copy(ds[t + 1][:, 448:], later[:, 448:])
+        make_d(PACK - 1, PACK + 1)
 
         for m0 in range(0, P, 32):
             round_part(nc.scalar.copy, w3_bf16, w3_raw, m0, m0, 32)
 
-        from_d = []
-        for t in range(PACK):
-            got = sb.tile([P, W], F32, name="from_d%d" % t)
-            nc.vector.tensor_copy(got[:], d[t][:].indirect(n2_t[:]))
-            from_d.append(got)
+        from_d = [sb.tile([P, W], F32, name="from_d0", tag="w1_bf16", align_bytes=64)]
+        from_d.extend(sb.tile([P, W], F32, name="from_d%d" % t) for t in range(1, PACK))
+
+        def fetch_d(t):
+            nc.vector.tensor_copy(from_d[t][:], d[t][:].indirect(n2_t[:]))
+
+        for t in range(PACK - 1):
+            fetch_d(t)
 
         z = sb.tile([P, S, PACK], BF16, name="z", align_bytes=64)
         from_y = []
@@ -134,14 +144,16 @@ def tile_picked_twlputbpagem_none_p_kernel(tc, x_words, x_scales, w1, w2, gn, w3
 
         def put_ra(t):
             nc.vector.tensor_tensor(ds[t][:].indirect(n1_t[:]), from_d[t][:], from_y[t][:], ADD)
-            for a, b in ((0, S),) if t + 1 < PACK else ((0, FIRST), (FIRST, S)):
+            for a, b in ((0, S),) if t + 1 < PACK else ((0, FIRST), (FIRST, 2 * FIRST), (2 * FIRST, S)):
                 nc.scalar.activation(z[:, a:b, t], ds[t][:, a:b], COPY, scale=gain[:, t : t + 1])
 
-        fetch_y(0)
-        for t in range(PACK):
-            if t + 1 < PACK:
-                fetch_y(t + 1)
+        for t in range(0, PACK, 2):
+            if t > 0:
+                fetch_d(PACK - 1)
+            fetch_y(t)
+            fetch_y(t + 1)
             put_ra(t)
+            put_ra(t + 1)
         w3_q = quantize(w3_bf16, "w3")
 
         z_flat = z[:].rearrange("p s t -> p (s t)")

from contextlib import ExitStack

import concourse.mybir as mybir

K, T, S, N, H, W, U = 512, 2048, 512, 512, 512, 256, 1024
FLOPS = 2 * K * H * S * 2 + 2 * H * N * S

F32 = mybir.dt.float32
BF16 = mybir.dt.bfloat16
I32 = mybir.dt.int32
U32 = mybir.dt.uint32
U16 = mybir.dt.uint16
U8 = mybir.dt.uint8
FP8X4 = mybir.dt.float8_e4m3fn_x4
MULT = mybir.AluOpType.mult
ADD = mybir.AluOpType.add
COPY = mybir.ActivationFunctionType.Copy

P = 128
PACK = 4
HALF = 256
FIRST = 128


def tile_picked_twlputbpagem_none_p_kernel(tc, x_words, x_scales, w1, w2, gn, w3, mem, offs, two, n1, n2, n3, n4, out):
    nc = tc.nc
    with ExitStack() as ctx:
        lists = ctx.enter_context(tc.tile_pool(name="lists", bufs=1))
        sb = ctx.enter_context(tc.tile_pool(name="sb", bufs=1))
        psum = ctx.enter_context(tc.psum_pool(name="psum", bufs=1))

        def load_list(src, name):
            tile = lists.tile(list(src.shape), U16, name=name)
            nc.sync.dma_start(tile[:], src)
            return tile

        def load_weight(w, name):
            halves = []
            for h in range(2):
                raw = sb.tile([P, PACK, HALF], F32, name="%s_raw%d" % (name, h))
                queue = nc.scalar if (name, h) == ("w2", 0) else nc.sync
                queue.dma_start(raw[:], w[:, h * HALF : (h + 1) * HALF].rearrange("(p j) c -> p j c", j=PACK))
                halves.append(raw)
            return halves

        def round_part(copy, grouped, raw, m0, c0, count):
            dealt = grouped[:].rearrange("p (t m j) -> p m j t", t=PACK, j=PACK)
            copy(dealt[:, m0 : m0 + count], raw[:].rearrange("p j (m t) -> p m j t", t=PACK)[:, c0 : c0 + count])

        def quantize(grouped, name, step=512):
            codes = sb.tile([P, 512], U32, name=name + "_codes", align_bytes=64)
            scales = sb.tile([P, 512], U8, name=name + "_scales", align_bytes=64)
            for c in range(0, 512, step):
                nc.vector.quantize_mx(out=codes[:, c : c + step].bitcast(FP8X4), scales=scales[:, c : c + step], in_=grouped[:, PACK * c : PACK * (c + step)])
            return codes, scales

        def product(acc, weight, t, codes, scales):
            cols = slice(t * P, (t + 1) * P)
            nc.tensor.matmul_mx(out=acc, lhsT=weight[0][:, cols].bitcast(FP8X4), lhsT_scale=weight[1][:, cols],
                                rhs=codes.bitcast(FP8X4), rhs_scale=scales, start=True, stop=True)

        two_t = load_list(two, "two_t")
        offs_t = load_list(offs, "offs_t")
        xs = sb.tile([P, T], U8, name="xs", align_bytes=64)
        nc.vector.memset(xs[:].bitcast(I32), 0)
        for q in range(4):
            nc.sync.dma_start(xs[32 * q : 32 * q + 4, :].bitcast(I32), x_scales[0, 4 * q : 4 * q + 4, :].bitcast(I32))
        xw = sb.tile([P, T], I32, name="xw", align_bytes=64)
        nc.sync.dma_start(xw[:], x_words[0].rearrange("p c r -> p (c r)").bitcast(I32))
        w2_raw = load_weight(w2, "w2")
        w1_raw = load_weight(w1, "w1")
        n2_t = load_list(n2, "n2_t")
        n1_t = load_list(n1, "n1_t")
        gain = sb.tile([P, PACK], F32, name="gain")
        nc.sync.dma_start(gain[:], gn.rearrange("(p t) o -> p (t o)", t=PACK))
        w3_raw = sb.tile([P, PACK, N], F32, name="w3_raw")
        nc.sync.dma_start(w3_raw[:], w3.rearrange("(p j) c -> p j c", j=PACK))
        n3_t = load_list(n3, "n3_t")
        pg = []
        for t in range(PACK):
            page = sb.tile([P, U], F32, name="pg%d" % t)
            nc.sync.dma_start(page[:], mem.rearrange("(p t) w -> p t w", t=PACK)[:, t, :])
            pg.append(page)
        n4_t = load_list(n4, "n4_t")

        picked = {}
        for name, lst in (("two", two_t), ("offs", offs_t)):
            scales = sb.tile([P, S], U8, name=name + "_s", align_bytes=64)
            nc.vector.tensor_copy(scales[:], xs[:].indirect(lst[:]))
            picked[name + "_s"] = scales
        for name, lst in (("two", two_t), ("offs", offs_t)):
            words = sb.tile([P, S], U32, name=name + "_w", align_bytes=64)
            nc.vector.tensor_copy(words[:], xw[:].bitcast(U32).indirect(lst[:]))
            picked[name + "_w"] = words

        w2_bf16 = sb.tile([P, PACK * H], BF16, name="w2_bf16", align_bytes=64)
        w1_bf16 = sb.tile([P, PACK * H], BF16, name="w1_bf16", tag="w1_bf16", align_bytes=64)
        w3_bf16 = sb.tile([P, PACK * N], BF16, name="w3_bf16", align_bytes=64)
        round_part(nc.scalar.copy, w2_bf16, w2_raw[0], 0, 0, 64)
        round_part(nc.scalar.copy, w2_bf16, w2_raw[1], 64, 0, 64)
        round_part(nc.scalar.copy, w1_bf16, w1_raw[0], 0, 0, 64)
        w2_q = quantize(w2_bf16, "w2", 256)
        round_part(nc.vector.tensor_copy, w1_bf16, w1_raw[1], 64, 0, 64)
        d = [sb.tile([P, S], F32, name="d%d" % t) for t in range(PACK)]

        def make_d(t, bank):
            acc = psum.tile([P, S], F32, name="bank%d" % bank)
            product(acc[:], w2_q, t, picked["two_w"][:], picked["two_s"][:])
            nc.scalar.copy(d[t][:], acc[:])

        for t in range(PACK - 1):
            make_d(t, t)
        w1_q = quantize(w1_bf16, "w1", 256)
        ds = [sb.tile([P, S], F32, name="ds%d" % t) for t in range(PACK)]
        for t in range(0, PACK, 2):
            later = psum.tile([P, S], F32, name="bank%d" % (PACK + t + 1))
            product(later[:], w1_q, t + 1, picked["offs_w"][:], picked["offs_s"][:])
            first = psum.tile([P, S], F32, name="bank%d" % (PACK + t))
            product(first[:], w1_q, t, picked["offs_w"][:], picked["offs_s"][:])
            nc.scalar.copy(ds[t + 1][:, :448], later[:, :448])
            nc.scalar.copy(ds[t][:], first[:])
            nc.scalar.copy(ds[t + 1][:, 448:], later[:, 448:])
        make_d(PACK - 1, PACK + 1)

        for m0 in range(0, P, 32):
            round_part(nc.scalar.copy, w3_bf16, w3_raw, m0, m0, 32)

        from_d = [sb.tile([P, W], F32, name="from_d0", tag="w1_bf16", align_bytes=64)]
        from_d.extend(sb.tile([P, W], F32, name="from_d%d" % t) for t in range(1, PACK))

        def fetch_d(t):
            nc.vector.tensor_copy(from_d[t][:], d[t][:].indirect(n2_t[:]))

        for t in range(PACK - 1):
            fetch_d(t)

        z = sb.tile([P, S, PACK], BF16, name="z", align_bytes=64)
        from_y = []

        def fetch_y(t):
            got = sb.tile([P, W], F32, name="from_y%d" % t)
            nc.vector.tensor_scalar(got[:], ds[t][:].indirect(n1_t[:]), -0.5, 0.0, MULT, ADD)
            from_y.append(got)

        def put_ra(t):
            nc.vector.tensor_tensor(ds[t][:].indirect(n1_t[:]), from_d[t][:], from_y[t][:], ADD)
            for a, b in ((0, S),) if t + 1 < PACK else ((0, FIRST), (FIRST, 2 * FIRST), (2 * FIRST, S)):
                nc.scalar.activation(z[:, a:b, t], ds[t][:, a:b], COPY, scale=gain[:, t : t + 1])

        for t in range(0, PACK, 2):
            if t > 0:
                fetch_d(PACK - 1)
            fetch_y(t)
            fetch_y(t + 1)
            put_ra(t)
            put_ra(t + 1)
        w3_q = quantize(w3_bf16, "w3")

        z_flat = z[:].rearrange("p s t -> p (s t)")
        def quantize_z(a, b):
            codes = sb.tile([P, b - a], U32, name="z_codes%d" % a, align_bytes=64)
            scales = sb.tile([P, b - a], U8, name="z_scales%d" % a, align_bytes=64)
            nc.vector.quantize_mx(out=codes[:].bitcast(FP8X4), scales=scales[:], in_=z_flat[:, PACK * a : PACK * b])
            return a, b, codes, scales

        z_first = quantize_z(0, FIRST)
        h_first = []
        for t in range(PACK):
            acc = psum.tile([P, FIRST], F32, name="bank%d" % t)
            product(acc[:], w3_q, t, z_first[2][:], z_first[3][:])
            row = sb.tile([P, FIRST], F32, name="h_first%d" % t)
            if t == 0:
                nc.vector.tensor_copy(row[:], acc[:])
            else:
                nc.scalar.copy(row[:], acc[:])
            h_first.append(row)
        nc.vector.tensor_copy(pg[0][:].indirect(n3_t[:, : FIRST // 16]), h_first[0][:])
        z_rest = [quantize_z(128, 256), quantize_z(256, 512)]
        h_rest = []
        for t in range(PACK):
            acc = psum.tile([P, S], F32, name="bank%d" % (PACK + t))
            for a, b, codes, scales in z_rest:
                product(acc[:, a:b], w3_q, t, codes[:], scales[:])
            row = sb.tile([P, S - FIRST], F32, name="h_rest%d" % t)
            nc.scalar.copy(row[:], acc[:, FIRST:])
            h_rest.append(row)
        for t in range(1, PACK):
            nc.vector.tensor_copy(pg[t][:].indirect(n3_t[:, : FIRST // 16]), h_first[t][:])

        half = []
        out_rows = out.rearrange("(p t) w -> p t w", t=PACK)

        def put_h(t):
            nc.vector.tensor_copy(pg[t][:].indirect(n3_t[:, FIRST // 16 :]), h_rest[t][:])
            scaled = sb.tile([P, U], F32, name="half%d" % t)
            nc.scalar.mul(scaled[:], pg[t][:], -0.5)
            half.append(scaled)

        def finish(t):
            cuts = (0, 512, 1024) if t + 1 < PACK else (0, 512, 768, 1024)
            for a, b in zip(cuts[:-1], cuts[1:]):
                res = sb.tile([P, b - a], F32, name="res%d_%d" % (t, a))
                nc.vector.tensor_tensor(res[:], half[t][:].indirect(n4_t[:, a // 16 : b // 16]), pg[t][:, a:b], ADD)
                nc.sync.dma_start(out_rows[:, t, a:b], res[:])

        put_h(0)
        for t in range(PACK):
            if t + 1 < PACK:
                put_h(t + 1)
            finish(t)
